import numpy as np
import ml_dtypes

BF16 = ml_dtypes.bfloat16


def bf(x):
    return np.asarray(x, np.float32).astype(BF16)


def f32(x):
    return np.asarray(x, np.float32)


def f64(x):
    return np.asarray(x).astype(np.float64)


def striped(idx):
    return np.concatenate([l.reshape(-1, 16).T for l in idx])


def rows(idx, k):
    return np.tile(np.repeat(idx, 16, axis=0), (k // (16 * 8), 1))


def look(tab, idx):
    return np.take_along_axis(f64(tab), rows(idx, len(tab)), axis=1)


K, S, V, N, M = 128, 2048, 512, 512, 128


def setup_inputs():
    return {"tab": f32(np.random.standard_normal((K, S))), "qry": f32(np.random.standard_normal((K, V))), "w": bf(np.random.uniform(0.0, 2.0, (K, M)) / K), "offs": striped(np.random.randint(0, S, (8, N)))}


def reference(tab, qry, w, offs):
    idx = np.stack([g.T.reshape(-1) for g in np.split(offs, 8)])
    x = np.abs(look(tab, idx) - f64(qry))
    y = f64(w).T @ x
    return y

@@ -1,0 +1,37 @@
+import concourse.mybir as mybir
+
+ROWS, TABLE_COLS, QUERIES, METRICS = 128, 2048, 512, 128
+GROUP = 16
+
+FLOPS = 2 * ROWS * METRICS * QUERIES
+
+F32, BF16, U16 = mybir.dt.float32, mybir.dt.bfloat16, mybir.dt.uint16
+
+
+def tile_lookup_manh_sub_none_kernel(tc, tab, qry, w, offs, out):
+    nc = tc.nc
+    with (
+        tc.tile_pool(name="sbuf", bufs=1) as sbuf,
+        tc.psum_pool(name="psum", bufs=1) as psum,
+    ):
+        offsets = sbuf.tile([ROWS, QUERIES // GROUP], U16, name="offsets")
+        table = sbuf.tile([ROWS, TABLE_COLS], F32, name="table")
+        queries = sbuf.tile([ROWS, QUERIES], F32, name="queries")
+        weights = sbuf.tile([ROWS, METRICS], BF16, name="weights")
+        nc.sync.dma_start(offsets[:], offs)
+        nc.sync.dma_start(table[:], tab)
+        nc.sync.dma_start(queries[:], qry)
+        nc.sync.dma_start(weights[:], w)
+
+        diff = sbuf.tile([ROWS, QUERIES], F32, name="diff")
+        nc.vector.tensor_tensor(diff[:], table[:].indirect(offsets[:]), queries[:], mybir.AluOpType.subtract)
+
+        dist = sbuf.tile([ROWS, QUERIES], BF16, name="dist")
+        nc.scalar.activation(dist[:], diff[:], mybir.ActivationFunctionType.Abs)
+
+        product = psum.tile([METRICS, QUERIES], F32, name="product")
+        nc.tensor.matmul(product[:], weights[:], dist[:], start=True, stop=True)
+
+        result = sbuf.tile([METRICS, QUERIES], F32, name="result")
+        nc.vector.tensor_copy(result[:], product[:])
+        nc.sync.dma_start(out, result[:])

@@ -2,10 +2,12 @@ import concourse.mybir as mybir
 
 ROWS, TABLE_COLS, QUERIES, METRICS = 128, 2048, 512, 128
 GROUP = 16
+HALF = QUERIES // 2
 
 FLOPS = 2 * ROWS * METRICS * QUERIES
 
 F32, BF16, U16 = mybir.dt.float32, mybir.dt.bfloat16, mybir.dt.uint16
+ALU = mybir.AluOpType
 
 
 def tile_lookup_manh_sub_none_kernel(tc, tab, qry, w, offs, out):
@@ -18,20 +20,30 @@ def tile_lookup_manh_sub_none_kernel(tc, tab, qry, w, offs, out):
         table = sbuf.tile([ROWS, TABLE_COLS], F32, name="table")
         queries = sbuf.tile([ROWS, QUERIES], F32, name="queries")
         weights = sbuf.tile([ROWS, METRICS], BF16, name="weights")
+        mid = TABLE_COLS // 2
+        nc.sync.dma_start(table[:, :mid], tab[:, :mid])
+        nc.scalar.dma_start(table[:, mid:], tab[:, mid:])
         nc.sync.dma_start(offsets[:], offs)
-        nc.sync.dma_start(table[:], tab)
-        nc.sync.dma_start(queries[:], qry)
+        nc.scalar.dma_start(queries[:], qry)
         nc.sync.dma_start(weights[:], w)
 
         diff = sbuf.tile([ROWS, QUERIES], F32, name="diff")
-        nc.vector.tensor_tensor(diff[:], table[:].indirect(offsets[:]), queries[:], mybir.AluOpType.subtract)
+        nc.vector.tensor_tensor(diff[:], table[:].indirect(offsets[:]), queries[:], ALU.subtract)
 
-        dist = sbuf.tile([ROWS, QUERIES], BF16, name="dist")
-        nc.scalar.activation(dist[:], diff[:], mybir.ActivationFunctionType.Abs)
+        low, high = slice(0, HALF), slice(HALF, QUERIES)
+        dist_low = sbuf.tile([ROWS, HALF], BF16, name="dist_low")
+        dist_high = sbuf.tile([ROWS, HALF], BF16, name="dist_high")
+        nc.scalar.activation(dist_low[:], diff[:, low], mybir.ActivationFunctionType.Abs)
+        nc.vector.scalar_tensor_tensor(dist_high[:], diff[:, high], -1.0, diff[:, high], ALU.mult, ALU.max)
 
-        product = psum.tile([METRICS, QUERIES], F32, name="product")
-        nc.tensor.matmul(product[:], weights[:], dist[:], start=True, stop=True)
+        product_low = psum.tile([METRICS, HALF], F32, name="product_low")
+        product_high = psum.tile([METRICS, HALF], F32, name="product_high")
+        nc.tensor.matmul(product_low[:], weights[:], dist_low[:], start=True, stop=True)
+        nc.tensor.matmul(product_high[:], weights[:], dist_high[:], start=True, stop=True)
 
-        result = sbuf.tile([METRICS, QUERIES], F32, name="result")
-        nc.vector.tensor_copy(result[:], product[:])
-        nc.sync.dma_start(out, result[:])
+        result_low = sbuf.tile([METRICS, HALF], F32, name="result_low")
+        result_high = sbuf.tile([METRICS, HALF], F32, name="result_high")
+        nc.scalar.copy(result_low[:], product_low[:])
+        nc.vector.tensor_copy(result_high[:], product_high[:])
+        nc.scalar.dma_start(out[:, low], result_low[:])
+        nc.sync.dma_start(out[:, high], result_high[:])

@@ -2,7 +2,8 @@ import concourse.mybir as mybir
 
 ROWS, TABLE_COLS, QUERIES, METRICS = 128, 2048, 512, 128
 GROUP = 16
-HALF = QUERIES // 2
+PIECES = 4
+PIECE = QUERIES // PIECES
 
 FLOPS = 2 * ROWS * METRICS * QUERIES
 
@@ -30,20 +31,20 @@ def tile_lookup_manh_sub_none_kernel(tc, tab, qry, w, offs, out):
         diff = sbuf.tile([ROWS, QUERIES], F32, name="diff")
         nc.vector.tensor_tensor(diff[:], table[:].indirect(offsets[:]), queries[:], ALU.subtract)
 
-        low, high = slice(0, HALF), slice(HALF, QUERIES)
-        dist_low = sbuf.tile([ROWS, HALF], BF16, name="dist_low")
-        dist_high = sbuf.tile([ROWS, HALF], BF16, name="dist_high")
-        nc.scalar.activation(dist_low[:], diff[:, low], mybir.ActivationFunctionType.Abs)
-        nc.vector.scalar_tensor_tensor(dist_high[:], diff[:, high], -1.0, diff[:, high], ALU.mult, ALU.max)
-
-        product_low = psum.tile([METRICS, HALF], F32, name="product_low")
-        product_high = psum.tile([METRICS, HALF], F32, name="product_high")
-        nc.tensor.matmul(product_low[:], weights[:], dist_low[:], start=True, stop=True)
-        nc.tensor.matmul(product_high[:], weights[:], dist_high[:], start=True, stop=True)
-
-        result_low = sbuf.tile([METRICS, HALF], F32, name="result_low")
-        result_high = sbuf.tile([METRICS, HALF], F32, name="result_high")
-        nc.scalar.copy(result_low[:], product_low[:])
-        nc.vector.tensor_copy(result_high[:], product_high[:])
-        nc.scalar.dma_start(out[:, low], result_low[:])
-        nc.sync.dma_start(out[:, high], result_high[:])
+        columns = [slice(k * PIECE, (k + 1) * PIECE) for k in range(PIECES)]
+        dist = [sbuf.tile([ROWS, PIECE], BF16, name=f"dist{k}") for k in range(PIECES)]
+        product = [psum.tile([METRICS, PIECE], F32, name=f"product{k}") for k in range(PIECES)]
+        result = [sbuf.tile([METRICS, PIECE], F32, name=f"result{k}") for k in range(PIECES)]
+        for k, cols in enumerate(columns):
+            if k % 2 == 0:
+                nc.scalar.activation(dist[k][:], diff[:, cols], mybir.ActivationFunctionType.Abs)
+            else:
+                nc.vector.scalar_tensor_tensor(dist[k][:], diff[:, cols], -1.0, diff[:, cols], ALU.mult, ALU.max)
+        for k in range(PIECES):
+            nc.tensor.matmul(product[k][:], weights[:], dist[k][:], start=True, stop=True)
+        for k, cols in enumerate(columns):
+            if k % 2 == 0:
+                nc.scalar.copy(result[k][:], product[k][:])
+            else:
+                nc.vector.tensor_copy(result[k][:], product[k][:])
+            nc.sync.dma_start(out[:, cols], result[k][:])

@@ -2,8 +2,9 @@ import concourse.mybir as mybir
 
 ROWS, TABLE_COLS, QUERIES, METRICS = 128, 2048, 512, 128
 GROUP = 16
-PIECES = 4
+PIECES = 2
 PIECE = QUERIES // PIECES
+WARM_UP = 14
 
 FLOPS = 2 * ROWS * METRICS * QUERIES
 
@@ -28,6 +29,12 @@ def tile_lookup_manh_sub_none_kernel(tc, tab, qry, w, offs, out):
         nc.scalar.dma_start(queries[:], qry)
         nc.sync.dma_start(weights[:], w)
 
+        zeros = sbuf.tile([ROWS, QUERIES], BF16, name="zeros")
+        unused = psum.tile([ROWS, QUERIES], F32, name="unused")
+        nc.vector.memset(zeros[:], 0.0)
+        for step in range(WARM_UP):
+            nc.tensor.matmul(unused[:], zeros[:, :ROWS], zeros[:], start=step == 0, stop=step == WARM_UP - 1)
+
         diff = sbuf.tile([ROWS, QUERIES], F32, name="diff")
         nc.vector.tensor_tensor(diff[:], table[:].indirect(offsets[:]), queries[:], ALU.subtract)
 
@@ -47,4 +54,5 @@ def tile_lookup_manh_sub_none_kernel(tc, tab, qry, w, offs, out):
                 nc.scalar.copy(result[k][:], product[k][:])
             else:
                 nc.vector.tensor_copy(result[k][:], product[k][:])
-            nc.sync.dma_start(out[:, cols], result[k][:])
+            queue = nc.scalar if k % 2 == 0 else nc.sync
+            queue.dma_start(out[:, cols], result[k][:])

@@ -22,11 +22,9 @@ def tile_lookup_manh_sub_none_kernel(tc, tab, qry, w, offs, out):
         table = sbuf.tile([ROWS, TABLE_COLS], F32, name="table")
         queries = sbuf.tile([ROWS, QUERIES], F32, name="queries")
         weights = sbuf.tile([ROWS, METRICS], BF16, name="weights")
-        mid = TABLE_COLS // 2
-        nc.sync.dma_start(table[:, :mid], tab[:, :mid])
-        nc.scalar.dma_start(table[:, mid:], tab[:, mid:])
-        nc.sync.dma_start(offsets[:], offs)
+        nc.sync.dma_start(table[:], tab)
         nc.scalar.dma_start(queries[:], qry)
+        nc.sync.dma_start(offsets[:], offs)
         nc.sync.dma_start(weights[:], w)
 
         zeros = sbuf.tile([ROWS, QUERIES], BF16, name="zeros")

import concourse.mybir as mybir

ROWS, TABLE_COLS, QUERIES, METRICS = 128, 2048, 512, 128
GROUP = 16
PIECES = 2
PIECE = QUERIES // PIECES
WARM_UP = 14

FLOPS = 2 * ROWS * METRICS * QUERIES

F32, BF16, U16 = mybir.dt.float32, mybir.dt.bfloat16, mybir.dt.uint16
ALU = mybir.AluOpType


def tile_lookup_manh_sub_none_kernel(tc, tab, qry, w, offs, out):
    nc = tc.nc
    with (
        tc.tile_pool(name="sbuf", bufs=1) as sbuf,
        tc.psum_pool(name="psum", bufs=1) as psum,
    ):
        offsets = sbuf.tile([ROWS, QUERIES // GROUP], U16, name="offsets")
        table = sbuf.tile([ROWS, TABLE_COLS], F32, name="table")
        queries = sbuf.tile([ROWS, QUERIES], F32, name="queries")
        weights = sbuf.tile([ROWS, METRICS], BF16, name="weights")
        nc.sync.dma_start(table[:], tab)
        nc.scalar.dma_start(queries[:], qry)
        nc.sync.dma_start(offsets[:], offs)
        nc.sync.dma_start(weights[:], w)

        zeros = sbuf.tile([ROWS, QUERIES], BF16, name="zeros")
        unused = psum.tile([ROWS, QUERIES], F32, name="unused")
        nc.vector.memset(zeros[:], 0.0)
        for step in range(WARM_UP):
            nc.tensor.matmul(unused[:], zeros[:, :ROWS], zeros[:], start=step == 0, stop=step == WARM_UP - 1)

        diff = sbuf.tile([ROWS, QUERIES], F32, name="diff")
        nc.vector.tensor_tensor(diff[:], table[:].indirect(offsets[:]), queries[:], ALU.subtract)

        columns = [slice(k * PIECE, (k + 1) * PIECE) for k in range(PIECES)]
        dist = [sbuf.tile([ROWS, PIECE], BF16, name=f"dist{k}") for k in range(PIECES)]
        product = [psum.tile([METRICS, PIECE], F32, name=f"product{k}") for k in range(PIECES)]
        result = [sbuf.tile([METRICS, PIECE], F32, name=f"result{k}") for k in range(PIECES)]
        for k, cols in enumerate(columns):
            if k % 2 == 0:
                nc.scalar.activation(dist[k][:], diff[:, cols], mybir.ActivationFunctionType.Abs)
            else:
                nc.vector.scalar_tensor_tensor(dist[k][:], diff[:, cols], -1.0, diff[:, cols], ALU.mult, ALU.max)
        for k in range(PIECES):
            nc.tensor.matmul(product[k][:], weights[:], dist[k][:], start=True, stop=True)
        for k, cols in enumerate(columns):
            if k % 2 == 0:
                nc.scalar.copy(result[k][:], product[k][:])
            else:
                nc.vector.tensor_copy(result[k][:], product[k][:])
            queue = nc.scalar if k % 2 == 0 else nc.sync
            queue.dma_start(out[:, cols], result[k][:])
